import numpy as np
import ml_dtypes


def mxq(x, axis, fmt="e4m3"):
    dtype, down = {"e4m3": (ml_dtypes.float8_e4m3fn, 7), "e5m2": (ml_dtypes.float8_e5m2, 14)}[fmt]
    v = np.moveaxis(np.asarray(x, np.float32).astype(ml_dtypes.bfloat16).astype(np.float64), axis, -1)
    blocks = v.reshape(v.shape[:-1] + (-1, 32))
    amax = np.abs(blocks).max(-1, keepdims=True)
    byte = np.maximum(np.where(amax > 0, np.frexp(amax)[1] - 1 + 127, 0) - down, 1)
    scale = np.exp2(byte - 127.0)
    codes = (blocks / scale).astype(np.float32).astype(dtype).astype(np.float64)
    return np.moveaxis((codes * scale).reshape(v.shape), -1, axis)


WIDE = False


def mx_kscale(k, group=512):
    if not WIDE:
        return np.ones(k)
    levels = np.array([18, -18])
    if group != 512:
        return np.exp2(np.random.permutation(np.resize(levels, k // group))).repeat(group)
    if k % 512:
        return np.exp2(np.random.permutation(np.resize(levels, k // 32))).repeat(32)
    a = np.empty((k // 512, 16))
    for p in range(k // 512):
        a[p, :8] = np.random.permutation(np.resize(levels, 8))
        for g in range(8):
            far = levels[np.abs(levels - a[p, g]) >= 10]
            a[p, g + 8] = far[np.random.randint(len(far))]
    return np.exp2(a.ravel()).repeat(32)


def f64(x):
    return np.asarray(x).astype(np.float64)


def sigmoid(v):
    return 1.0 / (1.0 + np.exp(-v))


def bf(x):
    return np.asarray(x, np.float32).astype(ml_dtypes.bfloat16)


def planes(Y):
    r, m = Y.shape
    b = f64(bf(Y)).reshape(r // 32, 32, m)
    amax = np.abs(b).max(1)
    byte = np.clip(np.where(amax > 0, np.frexp(amax)[1] - 1 + 127 - 7, 1), 1, 254)
    codes = (b * np.exp2(127.0 - byte)[:, None, :]).reshape(r, m).astype(np.float32).astype(ml_dtypes.float8_e4m3fn).view(np.uint8)
    words = codes.reshape(r // 512, 128, 4, m).transpose(0, 1, 3, 2)
    return np.ascontiguousarray(words), np.ascontiguousarray(byte.astype(np.uint8).reshape(r // 512, 16, m))


G, D, I, N, J = 4, 128, 128, 512, 128


def sgn(shape):
    return np.random.uniform(0.5, 2.0, shape) * np.where(np.random.standard_normal(shape) < 0, -1.0, 1.0)


def setup_inputs():
    n = np.random.standard_normal
    s_d = mx_kscale(D, 0)
    s_i = mx_kscale(I, 0)
    return {
        "x": (n((G, D, I)) * s_d[:, None]).astype(np.float32),
        "w": (n((D, N)) / np.sqrt(D) / s_d[:, None]).astype(np.float32),
        "ni": (sgn((G, I, 1)) * s_i[:, None]).astype(np.float32),
        "ad": ((np.random.uniform(size=(G, I, J)) < 0.1) * np.random.uniform(0.5, 1.0, (G, I, J)) / 3 / s_i[:, None]).astype(np.float32),
        "og": (n((G, J, N))).astype(np.float32),
        "r": (n((G, J, N))).astype(np.float32),
    }


def reference(x, w, ni, ad, og, r):
    xq = mxq(f64(x), 1, "e4m3")
    wq = mxq(f64(w), 0, "e4m3")
    z = xq.transpose(0, 2, 1) @ wq
    h = np.maximum(z, 0.0) * f64(ni)
    adq = mxq(f64(ad), 1, "e4m3")
    hq = mxq(h, 1, "e4m3")
    y = adq.transpose(0, 2, 1) @ hq
    out_ = y * sigmoid(f64(og)) + f64(r)
    Y = out_.reshape(G * J, N)
    words, scales = planes(Y)
    return Y, words, scales

@@ -1,0 +1,186 @@
+from contextlib import ExitStack
+
+import concourse.mybir as mybir
+
+G, D, I, N, J = 4, 128, 128, 512, 128
+FLOPS = 2 * G * D * I * N + 2 * G * I * J * N
+
+F32 = mybir.dt.float32
+BF16 = mybir.dt.bfloat16
+U32 = mybir.dt.uint32
+I32 = mybir.dt.int32
+U8 = mybir.dt.uint8
+FP8X4 = mybir.dt.float8_e4m3fn_x4
+ACT = mybir.ActivationFunctionType
+ALU = mybir.AluOpType
+
+P = 128
+ROWS = 32
+PACK = 4
+NM = 128
+HALF = N // 2
+V_COLS = 160
+
+
+def tile_rows_pl_gnn_gated_kernel(tc, x, w, ni, ad, og, r, out_0, out_1, out_2):
+    nc = tc.nc
+
+    def by_rows(ap):
+        return ap.rearrange("p t (c i) -> p c t i", i=4)
+
+    def by_words(ap):
+        return ap.rearrange("p (c i) t -> p c t i", i=4)
+
+    def pack_vector(dst, src):
+        nc.vector.tensor_copy(out=by_words(dst), in_=by_rows(src))
+
+    def pack_scalar(dst, src):
+        nc.scalar.activation(out=by_words(dst), in_=by_rows(src), func=ACT.Copy)
+
+    def quantize(codes, scales, packed):
+        nc.vector.quantize_mx(out=codes.bitcast(FP8X4), scales=scales, in_=packed.rearrange("p n t -> p (n t)"))
+
+    with ExitStack() as ctx:
+        sb = ctx.enter_context(tc.tile_pool(name="sb", bufs=1))
+        ps = ctx.enter_context(tc.psum_pool(name="ps", bufs=1))
+        ctx.enter_context(tc.manual_schedule())
+
+        def sbuf(name, shape, dtype):
+            return sb.tile(shape, dtype, name=name, align_bytes=64)
+
+        halves = range(2)
+        cols = [slice(h * HALF, (h + 1) * HALF) for h in halves]
+        bank = [[ps.tile([P, N], F32, name="bank%d_%d" % (h, g)) for g in range(G)] for h in halves]
+
+        x_raw = sbuf("x_raw", [P, PACK, I], F32)
+        w_raw = sbuf("w_raw", [P, PACK, N], F32)
+        ad_raw = sbuf("ad_raw", [P, PACK, J], F32)
+        ni_col = sbuf("ni_col", [P, G], F32)
+        og_raw = sbuf("og_raw", [P, G, N], F32)
+        r_raw = [sbuf("r_raw%d" % h, [P, PACK, HALF], F32) for h in halves]
+
+        x_rows = x.rearrange("g (p t) i -> (g p) t i", t=PACK)
+        w_rows = w.rearrange("(p t) n -> p t n", t=PACK)
+        nc.sync.dma_start(out=x_raw[64:128], in_=x_rows[64:128])
+        nc.scalar.dma_start(out=x_raw[0:64], in_=x_rows[0:64])
+        for g in range(G):
+            queue = nc.sync if g < 2 else nc.scalar
+            queue.dma_start(out=w_raw[ROWS * g : ROWS * (g + 1)], in_=w_rows)
+        with nc.allow_non_contiguous_dma(reason="one weight for each partition"):
+            nc.sync.dma_start(out=ni_col[:], in_=ni.rearrange("g i o -> i (g o)"))
+        nc.sync.dma_start(out=ad_raw[:], in_=ad.rearrange("g (p t) j -> (g p) t j", t=PACK))
+        nc.sync.dma_start(out=og_raw[:], in_=og.rearrange("g j n -> j g n"))
+
+        x_pk = sbuf("x_pk", [P, I, PACK], BF16)
+        x_codes = sbuf("x_codes", [P, I], U32)
+        x_scales = sbuf("x_scales", [P, I], U8)
+        pack_vector(x_pk[:], x_raw[:])
+        quantize(x_codes[:], x_scales[:], x_pk[:])
+
+        w_pk = [sbuf("w_pk%d" % h, [P, HALF, PACK], BF16) for h in halves]
+        w_codes = [sbuf("w_codes%d" % h, [P, HALF], U32) for h in halves]
+        w_scales = [sbuf("w_scales%d" % h, [P, HALF], U8) for h in halves]
+        for h in halves:
+            c0 = h * HALF
+            pack_vector(w_pk[h][:, :V_COLS, :], w_raw[:, :, c0 : c0 + V_COLS])
+            pack_scalar(w_pk[h][:, V_COLS:, :], w_raw[:, :, c0 + V_COLS : c0 + HALF])
+        for h in halves:
+            quantize(w_codes[h][:], w_scales[h][:], w_pk[h][:])
+
+        def products(h, st_codes, st_scales, mv_codes, mv_scales):
+            for c in range(HALF // NM):
+                cs = slice(c * NM, (c + 1) * NM)
+                for g in range(G):
+                    rows = slice(ROWS * g, ROWS * (g + 1))
+                    nc.tensor.matmul_mx(
+                        out=bank[h][g][:, cs],
+                        lhsT=st_codes[rows, :].bitcast(FP8X4),
+                        lhsT_scale=st_scales[rows, :],
+                        rhs=mv_codes[rows, cs].bitcast(FP8X4),
+                        rhs_scale=mv_scales[rows, cs],
+                        start=True,
+                        stop=True,
+                    )
+
+        h_rows = [sbuf("h_rows%d" % h, [P, PACK, HALF], BF16) for h in halves]
+        for h in halves:
+            products(h, x_codes, x_scales, w_codes[h], w_scales[h])
+        for h in halves:
+            h_nodes = [sbuf("h_nodes%d_%d" % (h, g), [P, HALF], BF16) for g in range(G)]
+            clipped = [sbuf("clipped%d_%d" % (h, g), [P, HALF], F32) for g in range(2)]
+            for g in (2, 3):
+                nc.scalar.activation(out=clipped[g - 2][:], in_=bank[h][g][:, :HALF], func=ACT.Relu)
+            for g in range(G):
+                if g < 2:
+                    nc.vector.tensor_scalar(
+                        out=h_nodes[g][:], in0=bank[h][g][:, :HALF], scalar1=0.0, scalar2=ni_col[:, g : g + 1],
+                        op0=ALU.max, op1=ALU.mult,
+                    )
+                else:
+                    nc.vector.tensor_scalar(
+                        out=h_nodes[g][:], in0=clipped[g - 2][:], scalar1=ni_col[:, g : g + 1], scalar2=None,
+                        op0=ALU.mult,
+                    )
+                nc.sync.dma_start(out=h_rows[h][ROWS * g : ROWS * (g + 1)], in_=h_nodes[g][:])
+
+        r_rows = r.rearrange("g (p u) n -> (g p) u n", u=PACK)
+        for h in halves:
+            nc.sync.dma_start(out=r_raw[h][:], in_=r_rows[:, :, cols[h]])
+
+        gate = [sbuf("gate%d" % h, [P, G, HALF], F32) for h in halves]
+
+        def gates(h):
+            nc.scalar.activation(out=gate[h][:], in_=og_raw[:, :, cols[h]], func=ACT.Tanh, scale=0.5)
+
+        ad_pk = sbuf("ad_pk", [P, J, PACK], BF16)
+        ad_codes = sbuf("ad_codes", [P, J], U32)
+        ad_scales = sbuf("ad_scales", [P, J], U8)
+        h_pk = [sbuf("h_pk%d" % h, [P, HALF, PACK], BF16) for h in halves]
+        h_codes = [sbuf("h_codes%d" % h, [P, HALF], U32) for h in halves]
+        h_scales = [sbuf("h_scales%d" % h, [P, HALF], U8) for h in halves]
+
+        gates(0)
+        pack_vector(ad_pk[:], ad_raw[:])
+        for h in halves:
+            pack_vector(h_pk[h][:, :V_COLS, :], h_rows[h][:, :, :V_COLS])
+            pack_scalar(h_pk[h][:, V_COLS:, :], h_rows[h][:, :, V_COLS:])
+            if h == 0:
+                quantize(ad_codes[:], ad_scales[:], ad_pk[:])
+            quantize(h_codes[h][:], h_scales[h][:], h_pk[h][:])
+            products(h, ad_codes, ad_scales, h_codes[h], h_scales[h])
+        gates(1)
+
+        m_rows = [sbuf("m_rows%d" % h, [P, PACK, HALF], F32) for h in halves]
+        for h in halves:
+            for g in range(G):
+                m_nodes = sbuf("m_nodes%d_%d" % (h, g), [P, HALF], F32)
+                nc.vector.scalar_tensor_tensor(
+                    out=m_nodes[:], in0=gate[h][:, g, :], scalar=1.0, in1=bank[h][g][:, :HALF],
+                    op0=ALU.add, op1=ALU.mult,
+                )
+                nc.sync.dma_start(out=m_rows[h][ROWS * g : ROWS * (g + 1)], in_=m_nodes[:])
+
+        out_rows = out_0.rearrange("(q u) n -> q u n", u=PACK)
+        words = out_1[0].rearrange("p n u -> p (n u)").bitcast(I32)
+        scale_rows = out_2[0].bitcast(I32)
+        o_pk = [sbuf("o_pk%d" % h, [P, HALF, PACK], BF16) for h in halves]
+        o_codes = [sbuf("o_codes%d" % h, [P, HALF], U32) for h in halves]
+        o_scales = sbuf("o_scales", [P, N], U8)
+        result = [sbuf("result%d" % h, [P, PACK, HALF], F32) for h in halves]
+        for h in halves:
+            nc.vector.scalar_tensor_tensor(
+                out=result[h][:].rearrange("p u n -> p (u n)"), in0=m_rows[h][:].rearrange("p u n -> p (u n)"),
+                scalar=0.5, in1=r_raw[h][:].rearrange("p u n -> p (u n)"), op0=ALU.mult, op1=ALU.add,
+            )
+            nc.sync.dma_start(out=out_rows[:, :, cols[h]], in_=result[h][:])
+            if h == 0:
+                pack_scalar(o_pk[0][:], result[0][:])
+        pack_scalar(o_pk[1][:, V_COLS:, :], result[1][:, :, V_COLS:])
+        quantize(o_codes[0][:], o_scales[:, cols[0]], o_pk[0][:])
+        nc.sync.dma_start(out=words[:, cols[0]], in_=o_codes[0][:].bitcast(I32))
+        pack_vector(o_pk[1][:, :V_COLS, :], result[1][:, :, :V_COLS])
+        quantize(o_codes[1][:], o_scales[:, cols[1]], o_pk[1][:])
+        nc.sync.dma_start(out=words[:, cols[1]], in_=o_codes[1][:].bitcast(I32))
+        for g in range(G):
+            queue = nc.sync if g < 2 else nc.scalar
+            queue.dma_start(out=scale_rows[4 * g : 4 * g + 4, :], in_=o_scales[ROWS * g : ROWS * g + 4, :].bitcast(I32))

@@ -32,10 +32,10 @@ def tile_rows_pl_gnn_gated_kernel(tc, x, w, ni, ad, og, r, out_0, out_1, out_2):
         return ap.rearrange("p (c i) t -> p c t i", i=4)
 
     def pack_vector(dst, src):
-        nc.vector.tensor_copy(out=by_words(dst), in_=by_rows(src))
+        nc.vector.tensor_copy(out=dst, in_=src.rearrange("p t n -> p n t"))
 
     def pack_scalar(dst, src):
-        nc.scalar.activation(out=by_words(dst), in_=by_rows(src), func=ACT.Copy)
+        nc.scalar.copy(out=dst, in_=src.rearrange("p t n -> p n t"))
 
     def quantize(codes, scales, packed):
         nc.vector.quantize_mx(out=codes.bitcast(FP8X4), scales=scales, in_=packed.rearrange("p n t -> p (n t)"))
@@ -53,21 +53,36 @@ def tile_rows_pl_gnn_gated_kernel(tc, x, w, ni, ad, og, r, out_0, out_1, out_2):
         bank = [[ps.tile([P, N], F32, name="bank%d_%d" % (h, g)) for g in range(G)] for h in halves]
 
         x_raw = sbuf("x_raw", [P, PACK, I], F32)
-        w_raw = sbuf("w_raw", [P, PACK, N], F32)
+        w_raw = [sbuf("w_raw%d" % h, [P, PACK, HALF], F32) for h in halves]
         ad_raw = sbuf("ad_raw", [P, PACK, J], F32)
-        ni_col = sbuf("ni_col", [P, G], F32)
+        warm = sbuf("warm", [P, 1], F32)
+        zero = sbuf("zero", [P, 1], F32)
+        ni_rows = sbuf("ni_rows", [P, G * ROWS], F32)
+        ni_cols = sbuf("ni_cols", [P, G * ROWS], F32)
         og_raw = sbuf("og_raw", [P, G, N], F32)
         r_raw = [sbuf("r_raw%d" % h, [P, PACK, HALF], F32) for h in halves]
 
         x_rows = x.rearrange("g (p t) i -> (g p) t i", t=PACK)
         w_rows = w.rearrange("(p t) n -> p t n", t=PACK)
-        nc.sync.dma_start(out=x_raw[64:128], in_=x_rows[64:128])
-        nc.scalar.dma_start(out=x_raw[0:64], in_=x_rows[0:64])
-        for g in range(G):
+
+        def load_w(h, g):
             queue = nc.sync if g < 2 else nc.scalar
-            queue.dma_start(out=w_raw[ROWS * g : ROWS * (g + 1)], in_=w_rows)
-        with nc.allow_non_contiguous_dma(reason="one weight for each partition"):
-            nc.sync.dma_start(out=ni_col[:], in_=ni.rearrange("g i o -> i (g o)"))
+            queue.dma_start(out=w_raw[h][ROWS * g : ROWS * (g + 1)], in_=w_rows[:, :, cols[h]])
+
+        nc.vector.memset(zero[:], 0.0)
+        nc.gpsimd.memset(ni_rows[:], 0.0)
+        nc.gpsimd.dma_start(
+            out=ni_rows[0:P:ROWS, :].rearrange("b (g q) -> b g q", g=G),
+            in_=ni.rearrange("g (b q) o -> b g (q o)", q=ROWS),
+        )
+        nc.sync.dma_start(out=x_raw[:], in_=x_rows)
+        for g in (2, 0, 3, 1):
+            load_w(0, g)
+        load_w(1, 2)
+        load_w(1, 3)
+        nc.scalar.activation(out=warm[:], in_=zero[:], func=ACT.Tanh)
+        load_w(1, 0)
+        load_w(1, 1)
         nc.sync.dma_start(out=ad_raw[:], in_=ad.rearrange("g (p t) j -> (g p) t j", t=PACK))
         nc.sync.dma_start(out=og_raw[:], in_=og.rearrange("g j n -> j g n"))
 
@@ -77,21 +92,11 @@ def tile_rows_pl_gnn_gated_kernel(tc, x, w, ni, ad, og, r, out_0, out_1, out_2):
         pack_vector(x_pk[:], x_raw[:])
         quantize(x_codes[:], x_scales[:], x_pk[:])
 
-        w_pk = [sbuf("w_pk%d" % h, [P, HALF, PACK], BF16) for h in halves]
-        w_codes = [sbuf("w_codes%d" % h, [P, HALF], U32) for h in halves]
-        w_scales = [sbuf("w_scales%d" % h, [P, HALF], U8) for h in halves]
-        for h in halves:
-            c0 = h * HALF
-            pack_vector(w_pk[h][:, :V_COLS, :], w_raw[:, :, c0 : c0 + V_COLS])
-            pack_scalar(w_pk[h][:, V_COLS:, :], w_raw[:, :, c0 + V_COLS : c0 + HALF])
-        for h in halves:
-            quantize(w_codes[h][:], w_scales[h][:], w_pk[h][:])
-
         def products(h, st_codes, st_scales, mv_codes, mv_scales):
-            for c in range(HALF // NM):
-                cs = slice(c * NM, (c + 1) * NM)
-                for g in range(G):
-                    rows = slice(ROWS * g, ROWS * (g + 1))
+            for g in range(G):
+                rows = slice(ROWS * g, ROWS * (g + 1))
+                for c in range(HALF // NM):
+                    cs = slice(c * NM, (c + 1) * NM)
                     nc.tensor.matmul_mx(
                         out=bank[h][g][:, cs],
                         lhsT=st_codes[rows, :].bitcast(FP8X4),
@@ -102,26 +107,46 @@ def tile_rows_pl_gnn_gated_kernel(tc, x, w, ni, ad, og, r, out_0, out_1, out_2):
                         stop=True,
                     )
 
+        w_pk = [sbuf("w_pk%d" % h, [P, HALF, PACK], BF16) for h in halves]
+        w_codes = [sbuf("w_codes%d" % h, [P, HALF], U32) for h in halves]
+        w_scales = [sbuf("w_scales%d" % h, [P, HALF], U8) for h in halves]
         h_rows = [sbuf("h_rows%d" % h, [P, PACK, HALF], BF16) for h in halves]
-        for h in halves:
+
+        def pack_w(h):
+            pack_vector(w_pk[h][:, :V_COLS, :], w_raw[h][:, :, :V_COLS])
+            pack_scalar(w_pk[h][:, V_COLS:, :], w_raw[h][:, :, V_COLS:])
+
+        def first_products(h):
+            quantize(w_codes[h][:], w_scales[h][:], w_pk[h][:])
             products(h, x_codes, x_scales, w_codes[h], w_scales[h])
+
+        clipped = {}
+
+        def clip(h, g):
+            clipped[h, g] = sbuf("clipped%d_%d" % (h, g), [P, HALF], F32)
+            nc.scalar.activation(out=clipped[h, g][:], in_=bank[h][g][:, :HALF], func=ACT.Relu)
+
+        def messages(h, g):
+            h_nodes = sbuf("h_nodes%d_%d" % (h, g), [P, HALF], BF16)
+            weight = ni_cols[:, ROWS * g : ROWS * g + 1]
+            if (h, g) in clipped:
+                nc.vector.tensor_scalar(out=h_nodes[:], in0=clipped[h, g][:], scalar1=weight, scalar2=None, op0=ALU.mult)
+            else:
+                nc.vector.tensor_scalar(
+                    out=h_nodes[:], in0=bank[h][g][:, :HALF], scalar1=0.0, scalar2=weight, op0=ALU.max, op1=ALU.mult
+                )
+            nc.sync.dma_start(out=h_rows[h][ROWS * g : ROWS * (g + 1)], in_=h_nodes[:])
+
+        pack_w(0)
+        first_products(0)
+        pack_w(1)
+        nc.vector.transpose(out=ni_cols[:], in_=ni_rows[:])
+        first_products(1)
         for h in halves:
-            h_nodes = [sbuf("h_nodes%d_%d" % (h, g), [P, HALF], BF16) for g in range(G)]
-            clipped = [sbuf("clipped%d_%d" % (h, g), [P, HALF], F32) for g in range(2)]
-            for g in (2, 3):
-                nc.scalar.activation(out=clipped[g - 2][:], in_=bank[h][g][:, :HALF], func=ACT.Relu)
-            for g in range(G):
-                if g < 2:
-                    nc.vector.tensor_scalar(
-                        out=h_nodes[g][:], in0=bank[h][g][:, :HALF], scalar1=0.0, scalar2=ni_col[:, g : g + 1],
-                        op0=ALU.max, op1=ALU.mult,
-                    )
-                else:
-                    nc.vector.tensor_scalar(
-                        out=h_nodes[g][:], in0=clipped[g - 2][:], scalar1=ni_col[:, g : g + 1], scalar2=None,
-                        op0=ALU.mult,
-                    )
-                nc.sync.dma_start(out=h_rows[h][ROWS * g : ROWS * (g + 1)], in_=h_nodes[g][:])
+            clip(h, 0)
+            clip(h, 2)
+            for g in (1, 0, 3, 2):
+                messages(h, g)
 
         r_rows = r.rearrange("g (p u) n -> (g p) u n", u=PACK)
         for h in halves:
@@ -139,26 +164,38 @@ def tile_rows_pl_gnn_gated_kernel(tc, x, w, ni, ad, og, r, out_0, out_1, out_2):
         h_codes = [sbuf("h_codes%d" % h, [P, HALF], U32) for h in halves]
         h_scales = [sbuf("h_scales%d" % h, [P, HALF], U8) for h in halves]
 
-        gates(0)
-        pack_vector(ad_pk[:], ad_raw[:])
-        for h in halves:
-            pack_vector(h_pk[h][:, :V_COLS, :], h_rows[h][:, :, :V_COLS])
-            pack_scalar(h_pk[h][:, V_COLS:, :], h_rows[h][:, :, V_COLS:])
-            if h == 0:
-                quantize(ad_codes[:], ad_scales[:], ad_pk[:])
+        m_rows = [sbuf("m_rows%d" % h, [P, PACK, HALF], F32) for h in halves]
+
+        def second_products(h):
             quantize(h_codes[h][:], h_scales[h][:], h_pk[h][:])
             products(h, ad_codes, ad_scales, h_codes[h], h_scales[h])
-        gates(1)
 
-        m_rows = [sbuf("m_rows%d" % h, [P, PACK, HALF], F32) for h in halves]
-        for h in halves:
-            for g in range(G):
-                m_nodes = sbuf("m_nodes%d_%d" % (h, g), [P, HALF], F32)
-                nc.vector.scalar_tensor_tensor(
-                    out=m_nodes[:], in0=gate[h][:, g, :], scalar=1.0, in1=bank[h][g][:, :HALF],
-                    op0=ALU.add, op1=ALU.mult,
-                )
-                nc.sync.dma_start(out=m_rows[h][ROWS * g : ROWS * (g + 1)], in_=m_nodes[:])
+        def gated(h, g):
+            m_nodes = sbuf("m_nodes%d_%d" % (h, g), [P, HALF], F32)
+            nc.vector.scalar_tensor_tensor(
+                out=m_nodes[:], in0=gate[h][:, g, :], scalar=1.0, in1=bank[h][g][:, :HALF],
+                op0=ALU.add, op1=ALU.mult,
+            )
+            nc.sync.dma_start(out=m_rows[h][ROWS * g : ROWS * (g + 1)], in_=m_nodes[:])
+
+        gates(0)
+        pack_vector(ad_pk[:], ad_raw[:])
+        quantize(ad_codes[:], ad_scales[:], ad_pk[:])
+        pack_vector(h_pk[0][:, :160, :], h_rows[0][:, :, :160])
+        pack_scalar(h_pk[0][:, 160:, :], h_rows[0][:, :, 160:])
+        second_products(0)
+        pack_vector(h_pk[1][:, :160, :], h_rows[1][:, :, :160])
+        pack_scalar(h_pk[1][:, 160:, :], h_rows[1][:, :, 160:])
+        gates(1)
+        gated(0, 0)
+        second_products(1)
+        gated(0, 1)
+        gated(0, 2)
+        gated(0, 3)
+        gated(1, 0)
+        gated(1, 1)
+        gated(1, 2)
+        gated(1, 3)
 
         out_rows = out_0.rearrange("(q u) n -> q u n", u=PACK)
         words = out_1[0].rearrange("p n u -> p (n u)").bitcast(I32)
@@ -167,18 +204,18 @@ def tile_rows_pl_gnn_gated_kernel(tc, x, w, ni, ad, og, r, out_0, out_1, out_2):
         o_codes = [sbuf("o_codes%d" % h, [P, HALF], U32) for h in halves]
         o_scales = sbuf("o_scales", [P, N], U8)
         result = [sbuf("result%d" % h, [P, PACK, HALF], F32) for h in halves]
-        for h in halves:
-            nc.vector.scalar_tensor_tensor(
-                out=result[h][:].rearrange("p u n -> p (u n)"), in0=m_rows[h][:].rearrange("p u n -> p (u n)"),
-                scalar=0.5, in1=r_raw[h][:].rearrange("p u n -> p (u n)"), op0=ALU.mult, op1=ALU.add,
-            )
-            nc.sync.dma_start(out=out_rows[:, :, cols[h]], in_=result[h][:])
-            if h == 0:
-                pack_scalar(o_pk[0][:], result[0][:])
-        pack_scalar(o_pk[1][:, V_COLS:, :], result[1][:, :, V_COLS:])
+        nc.vector.scalar_tensor_tensor(out=result[0][:, :, 0:128], in0=m_rows[0][:, :, 0:128], scalar=0.5, in1=r_raw[0][:, :, 0:128], op0=ALU.mult, op1=ALU.add)
+        pack_scalar(o_pk[0][:, 0:128, :], result[0][:, :, 0:128])
+        nc.vector.scalar_tensor_tensor(out=result[0][:, :, 128:256], in0=m_rows[0][:, :, 128:256], scalar=0.5, in1=r_raw[0][:, :, 128:256], op0=ALU.mult, op1=ALU.add)
+        nc.sync.dma_start(out=out_rows[:, :, cols[0]], in_=result[0][:])
+        pack_scalar(o_pk[0][:, 128:256, :], result[0][:, :, 128:256])
+        nc.vector.scalar_tensor_tensor(out=result[1][:, :, 0:128], in0=m_rows[1][:, :, 0:128], scalar=0.5, in1=r_raw[1][:, :, 0:128], op0=ALU.mult, op1=ALU.add)
+        pack_scalar(o_pk[1][:, 0:128, :], result[1][:, :, 0:128])
+        nc.vector.scalar_tensor_tensor(out=result[1][:, :, 128:256], in0=m_rows[1][:, :, 128:256], scalar=0.5, in1=r_raw[1][:, :, 128:256], op0=ALU.mult, op1=ALU.add)
+        nc.sync.dma_start(out=out_rows[:, :, cols[1]], in_=result[1][:])
         quantize(o_codes[0][:], o_scales[:, cols[0]], o_pk[0][:])
         nc.sync.dma_start(out=words[:, cols[0]], in_=o_codes[0][:].bitcast(I32))
-        pack_vector(o_pk[1][:, :V_COLS, :], result[1][:, :, :V_COLS])
+        pack_vector(o_pk[1][:, 128:256, :], result[1][:, :, 128:256])
         quantize(o_codes[1][:], o_scales[:, cols[1]], o_pk[1][:])
         nc.sync.dma_start(out=words[:, cols[1]], in_=o_codes[1][:].bitcast(I32))
         for g in range(G):

from contextlib import ExitStack

import concourse.mybir as mybir

G, D, I, N, J = 4, 128, 128, 512, 128
FLOPS = 2 * G * D * I * N + 2 * G * I * J * N

F32 = mybir.dt.float32
BF16 = mybir.dt.bfloat16
U32 = mybir.dt.uint32
I32 = mybir.dt.int32
U8 = mybir.dt.uint8
FP8X4 = mybir.dt.float8_e4m3fn_x4
ACT = mybir.ActivationFunctionType
ALU = mybir.AluOpType

P = 128
ROWS = 32
PACK = 4
NM = 128
HALF = N // 2
V_COLS = 160


def tile_rows_pl_gnn_gated_kernel(tc, x, w, ni, ad, og, r, out_0, out_1, out_2):
    nc = tc.nc

    def by_rows(ap):
        return ap.rearrange("p t (c i) -> p c t i", i=4)

    def by_words(ap):
        return ap.rearrange("p (c i) t -> p c t i", i=4)

    def pack_vector(dst, src):
        nc.vector.tensor_copy(out=dst, in_=src.rearrange("p t n -> p n t"))

    def pack_scalar(dst, src):
        nc.scalar.copy(out=dst, in_=src.rearrange("p t n -> p n t"))

    def quantize(codes, scales, packed):
        nc.vector.quantize_mx(out=codes.bitcast(FP8X4), scales=scales, in_=packed.rearrange("p n t -> p (n t)"))

    with ExitStack() as ctx:
        sb = ctx.enter_context(tc.tile_pool(name="sb", bufs=1))
        ps = ctx.enter_context(tc.psum_pool(name="ps", bufs=1))
        ctx.enter_context(tc.manual_schedule())

        def sbuf(name, shape, dtype):
            return sb.tile(shape, dtype, name=name, align_bytes=64)

        halves = range(2)
        cols = [slice(h * HALF, (h + 1) * HALF) for h in halves]
        bank = [[ps.tile([P, N], F32, name="bank%d_%d" % (h, g)) for g in range(G)] for h in halves]

        x_raw = sbuf("x_raw", [P, PACK, I], F32)
        w_raw = [sbuf("w_raw%d" % h, [P, PACK, HALF], F32) for h in halves]
        ad_raw = sbuf("ad_raw", [P, PACK, J], F32)
        warm = sbuf("warm", [P, 1], F32)
        zero = sbuf("zero", [P, 1], F32)
        ni_rows = sbuf("ni_rows", [P, G * ROWS], F32)
        ni_cols = sbuf("ni_cols", [P, G * ROWS], F32)
        og_raw = sbuf("og_raw", [P, G, N], F32)
        r_raw = [sbuf("r_raw%d" % h, [P, PACK, HALF], F32) for h in halves]

        x_rows = x.rearrange("g (p t) i -> (g p) t i", t=PACK)
        w_rows = w.rearrange("(p t) n -> p t n", t=PACK)

        def load_w(h, g):
            queue = nc.sync if g < 2 else nc.scalar
            queue.dma_start(out=w_raw[h][ROWS * g : ROWS * (g + 1)], in_=w_rows[:, :, cols[h]])

        nc.vector.memset(zero[:], 0.0)
        nc.gpsimd.memset(ni_rows[:], 0.0)
        nc.gpsimd.dma_start(
            out=ni_rows[0:P:ROWS, :].rearrange("b (g q) -> b g q", g=G),
            in_=ni.rearrange("g (b q) o -> b g (q o)", q=ROWS),
        )
        nc.sync.dma_start(out=x_raw[:], in_=x_rows)
        for g in (2, 0, 3, 1):
            load_w(0, g)
        load_w(1, 2)
        load_w(1, 3)
        nc.scalar.activation(out=warm[:], in_=zero[:], func=ACT.Tanh)
        load_w(1, 0)
        load_w(1, 1)
        nc.sync.dma_start(out=ad_raw[:], in_=ad.rearrange("g (p t) j -> (g p) t j", t=PACK))
        nc.sync.dma_start(out=og_raw[:], in_=og.rearrange("g j n -> j g n"))

        x_pk = sbuf("x_pk", [P, I, PACK], BF16)
        x_codes = sbuf("x_codes", [P, I], U32)
        x_scales = sbuf("x_scales", [P, I], U8)
        pack_vector(x_pk[:], x_raw[:])
        quantize(x_codes[:], x_scales[:], x_pk[:])

        def products(h, st_codes, st_scales, mv_codes, mv_scales):
            for g in range(G):
                rows = slice(ROWS * g, ROWS * (g + 1))
                for c in range(HALF // NM):
                    cs = slice(c * NM, (c + 1) * NM)
                    nc.tensor.matmul_mx(
                        out=bank[h][g][:, cs],
                        lhsT=st_codes[rows, :].bitcast(FP8X4),
                        lhsT_scale=st_scales[rows, :],
                        rhs=mv_codes[rows, cs].bitcast(FP8X4),
                        rhs_scale=mv_scales[rows, cs],
                        start=True,
                        stop=True,
                    )

        w_pk = [sbuf("w_pk%d" % h, [P, HALF, PACK], BF16) for h in halves]
        w_codes = [sbuf("w_codes%d" % h, [P, HALF], U32) for h in halves]
        w_scales = [sbuf("w_scales%d" % h, [P, HALF], U8) for h in halves]
        h_rows = [sbuf("h_rows%d" % h, [P, PACK, HALF], BF16) for h in halves]

        def pack_w(h):
            pack_vector(w_pk[h][:, :V_COLS, :], w_raw[h][:, :, :V_COLS])
            pack_scalar(w_pk[h][:, V_COLS:, :], w_raw[h][:, :, V_COLS:])

        def first_products(h):
            quantize(w_codes[h][:], w_scales[h][:], w_pk[h][:])
            products(h, x_codes, x_scales, w_codes[h], w_scales[h])

        clipped = {}

        def clip(h, g):
            clipped[h, g] = sbuf("clipped%d_%d" % (h, g), [P, HALF], F32)
            nc.scalar.activation(out=clipped[h, g][:], in_=bank[h][g][:, :HALF], func=ACT.Relu)

        def messages(h, g):
            h_nodes = sbuf("h_nodes%d_%d" % (h, g), [P, HALF], BF16)
            weight = ni_cols[:, ROWS * g : ROWS * g + 1]
            if (h, g) in clipped:
                nc.vector.tensor_scalar(out=h_nodes[:], in0=clipped[h, g][:], scalar1=weight, scalar2=None, op0=ALU.mult)
            else:
                nc.vector.tensor_scalar(
                    out=h_nodes[:], in0=bank[h][g][:, :HALF], scalar1=0.0, scalar2=weight, op0=ALU.max, op1=ALU.mult
                )
            nc.sync.dma_start(out=h_rows[h][ROWS * g : ROWS * (g + 1)], in_=h_nodes[:])

        pack_w(0)
        first_products(0)
        pack_w(1)
        nc.vector.transpose(out=ni_cols[:], in_=ni_rows[:])
        first_products(1)
        for h in halves:
            clip(h, 0)
            clip(h, 2)
            for g in (1, 0, 3, 2):
                messages(h, g)

        r_rows = r.rearrange("g (p u) n -> (g p) u n", u=PACK)
        for h in halves:
            nc.sync.dma_start(out=r_raw[h][:], in_=r_rows[:, :, cols[h]])

        gate = [sbuf("gate%d" % h, [P, G, HALF], F32) for h in halves]

        def gates(h):
            nc.scalar.activation(out=gate[h][:], in_=og_raw[:, :, cols[h]], func=ACT.Tanh, scale=0.5)

        ad_pk = sbuf("ad_pk", [P, J, PACK], BF16)
        ad_codes = sbuf("ad_codes", [P, J], U32)
        ad_scales = sbuf("ad_scales", [P, J], U8)
        h_pk = [sbuf("h_pk%d" % h, [P, HALF, PACK], BF16) for h in halves]
        h_codes = [sbuf("h_codes%d" % h, [P, HALF], U32) for h in halves]
        h_scales = [sbuf("h_scales%d" % h, [P, HALF], U8) for h in halves]

        m_rows = [sbuf("m_rows%d" % h, [P, PACK, HALF], F32) for h in halves]

        def second_products(h):
            quantize(h_codes[h][:], h_scales[h][:], h_pk[h][:])
            products(h, ad_codes, ad_scales, h_codes[h], h_scales[h])

        def gated(h, g):
            m_nodes = sbuf("m_nodes%d_%d" % (h, g), [P, HALF], F32)
            nc.vector.scalar_tensor_tensor(
                out=m_nodes[:], in0=gate[h][:, g, :], scalar=1.0, in1=bank[h][g][:, :HALF],
                op0=ALU.add, op1=ALU.mult,
            )
            nc.sync.dma_start(out=m_rows[h][ROWS * g : ROWS * (g + 1)], in_=m_nodes[:])

        gates(0)
        pack_vector(ad_pk[:], ad_raw[:])
        quantize(ad_codes[:], ad_scales[:], ad_pk[:])
        pack_vector(h_pk[0][:, :160, :], h_rows[0][:, :, :160])
        pack_scalar(h_pk[0][:, 160:, :], h_rows[0][:, :, 160:])
        second_products(0)
        pack_vector(h_pk[1][:, :160, :], h_rows[1][:, :, :160])
        pack_scalar(h_pk[1][:, 160:, :], h_rows[1][:, :, 160:])
        gates(1)
        gated(0, 0)
        second_products(1)
        gated(0, 1)
        gated(0, 2)
        gated(0, 3)
        gated(1, 0)
        gated(1, 1)
        gated(1, 2)
        gated(1, 3)

        out_rows = out_0.rearrange("(q u) n -> q u n", u=PACK)
        words = out_1[0].rearrange("p n u -> p (n u)").bitcast(I32)
        scale_rows = out_2[0].bitcast(I32)
        o_pk = [sbuf("o_pk%d" % h, [P, HALF, PACK], BF16) for h in halves]
        o_codes = [sbuf("o_codes%d" % h, [P, HALF], U32) for h in halves]
        o_scales = sbuf("o_scales", [P, N], U8)
        result = [sbuf("result%d" % h, [P, PACK, HALF], F32) for h in halves]
        nc.vector.scalar_tensor_tensor(out=result[0][:, :, 0:128], in0=m_rows[0][:, :, 0:128], scalar=0.5, in1=r_raw[0][:, :, 0:128], op0=ALU.mult, op1=ALU.add)
        pack_scalar(o_pk[0][:, 0:128, :], result[0][:, :, 0:128])
        nc.vector.scalar_tensor_tensor(out=result[0][:, :, 128:256], in0=m_rows[0][:, :, 128:256], scalar=0.5, in1=r_raw[0][:, :, 128:256], op0=ALU.mult, op1=ALU.add)
        nc.sync.dma_start(out=out_rows[:, :, cols[0]], in_=result[0][:])
        pack_scalar(o_pk[0][:, 128:256, :], result[0][:, :, 128:256])
        nc.vector.scalar_tensor_tensor(out=result[1][:, :, 0:128], in0=m_rows[1][:, :, 0:128], scalar=0.5, in1=r_raw[1][:, :, 0:128], op0=ALU.mult, op1=ALU.add)
        pack_scalar(o_pk[1][:, 0:128, :], result[1][:, :, 0:128])
        nc.vector.scalar_tensor_tensor(out=result[1][:, :, 128:256], in0=m_rows[1][:, :, 128:256], scalar=0.5, in1=r_raw[1][:, :, 128:256], op0=ALU.mult, op1=ALU.add)
        nc.sync.dma_start(out=out_rows[:, :, cols[1]], in_=result[1][:])
        quantize(o_codes[0][:], o_scales[:, cols[0]], o_pk[0][:])
        nc.sync.dma_start(out=words[:, cols[0]], in_=o_codes[0][:].bitcast(I32))
        pack_vector(o_pk[1][:, 128:256, :], result[1][:, :, 128:256])
        quantize(o_codes[1][:], o_scales[:, cols[1]], o_pk[1][:])
        nc.sync.dma_start(out=words[:, cols[1]], in_=o_codes[1][:].bitcast(I32))
        for g in range(G):
            queue = nc.sync if g < 2 else nc.scalar
            queue.dma_start(out=scale_rows[4 * g : 4 * g + 4, :], in_=o_scales[ROWS * g : ROWS * g + 4, :].bitcast(I32))
